import numpy as np, ml_dtypes
CORES = [16,32,48,64,80]
N = 5
import mx_ref
NC, G = 256, 4
C = np.float32(0.041)
CNT = [[0,8,0,128,120],[56,0,32,104,64],[104,72,0,16,64],[16,72,168,0,0],[80,104,56,8,8]]
OFF = [[sum(c[:e]) for e in range(N + 1)] for c in CNT]
BF = ml_dtypes.bfloat16
def cut(t, i, w=512):
    return t[:, w * i:w * i + w]
def tile(rs):
    return np.stack(rs, axis=2).reshape(128, -1).astype(BF)
def layer(w, X):
    out = []
    for i in range(G):
        for t in range(len(X)):
            p = mx_ref.matmul(mx_ref.quantize(cut(w, len(X) * i + t)), X[t])
            z = p if t == 0 else z + p
        out.append(z)
    return out
def act(Z):
    return [np.maximum(z, 0) * C for z in Z]
def setup_inputs(rng):
    def f(*shape):
        return mx_ref.flush((rng.standard_normal(shape, dtype=np.float32) * np.exp2(rng.integers(-2, 3, shape[:-1] + (1,)))).astype(BF))
    return {"x": f(N, 128, 4 * NC), "w1": f(N, 128, G * 512), "w2": f(N, 128, 512)}
def setup_inputs_blocks(rng):
    d = setup_inputs(rng)
    for k in ("x", "w1", "w2"): d[k] = mx_ref.spread(d[k], rng, 4)
    return d
def setup_inputs_wide(rng):
    d = setup_inputs(rng)
    for k in ("x", "w1", "w2"): d[k] = mx_ref.flush((d[k].astype(np.float32) * np.exp2(rng.integers(-8, 9, (N, 1, 1))).astype(np.float32)).astype(BF))
    return d
def setup_inputs_zeros(rng):
    d = setup_inputs(rng); v = d["x"].reshape(N, 128, -1, 4).copy()
    v[np.broadcast_to((rng.random((N, 1, v.shape[2], 1)) < 0.33), v.shape)] = 0
    d["x"] = v.reshape(d["x"].shape)
    return d
def reference(x, w1, w2):
    y = np.zeros((N, 128, NC), np.float32)
    for e in range(N):
        t = np.concatenate([x[j][:, 4 * OFF[j][e]:4 * OFF[j][e + 1]] for j in range(N)], axis=1)
        p = mx_ref.matmul(mx_ref.quantize(w2[e]), mx_ref.quantize(tile(act(layer(w1[e], [mx_ref.quantize(t)])))))
        y[e] = p
    return {"y": y}

@@ -1,0 +1,186 @@
+from concourse.mybir import dt, AluOpType, ActivationFunctionType
+
+NC = 256
+WIN = 128
+G = 4
+C = 0.041
+BANK = 512
+ROW = 512
+
+SCRATCH = {
+    "xb": ("sbuf", [128, 4 * NC], "bfloat16"),
+    "w1b": ("sbuf", [128, G * 512], "bfloat16"),
+    "w2b": ("sbuf", [128, 512], "bfloat16"),
+    "xq": ("sbuf", [128, NC], "float8_e4m3fn_x4"),
+    "xs": ("sbuf", [128, NC], "uint8"),
+    "w1q": ("sbuf", [128, G * 128], "float8_e4m3fn_x4"),
+    "w1s": ("sbuf", [128, G * 128], "uint8"),
+    "w2q": ("sbuf", [128, 128], "float8_e4m3fn_x4"),
+    "w2s": ("sbuf", [128, 128], "uint8"),
+    "bq": ("sbuf", [128, NC], "float8_e4m3fn_x4"),
+    "bs": ("sbuf", [128, NC], "uint8"),
+    "h": ("sbuf", [128, 4 * NC], "bfloat16"),
+    "hq": ("sbuf", [128, NC], "float8_e4m3fn_x4"),
+    "hs": ("sbuf", [128, NC], "uint8"),
+    "ys": ("sbuf", [128, NC], "float32"),
+    "ps": ("psum", [128, 8 * BANK], "float32"),
+}
+SEMAPHORES = (["ldx0", "ldx1", "ldw1", "ldw2", "qx0", "qx1", "qw1", "qw2", "arrA", "arrB", "sent",
+               "a0", "a1", "aown", "qh0", "qh1", "p0", "p1", "c0", "c1", "st"]
+              + ["z0%d" % b for b in range(G)] + ["z1%d" % b for b in range(G)] + ["zo%d" % b for b in range(G)])
+
+
+def _groups(mask, k):
+    bits = [i for i in range(16) if (mask >> i) & 1]
+    n = len(bits) // k
+    return [sum(1 << i for i in bits[t * n:(t + 1) * n]) for t in range(k)], n
+
+
+def _deal(loads):
+    best, pick = None, None
+    for m in range(1 << len(loads)):
+        s1 = sum(v for i, v in enumerate(loads) if (m >> i) & 1)
+        top = max(s1, sum(loads) - s1)
+        if best is None or top < best:
+            best, pick = top, m
+    return [(pick >> i) & 1 for i in range(len(loads))]
+
+
+def _plan(cnt, j):
+    n = len(cnt)
+    runs = []
+    for e in range(n):
+        if e != j and cnt[j][e]:
+            runs.append((e, sum(cnt[j][:e]), cnt[j][e], sum(cnt[k][e] for k in range(j))))
+    runs.sort(key=lambda r: (r[1] + r[2] > WIN, r[3] >= WIN, r[1]))
+    return runs
+
+
+def rank_program(g, core, T, topo):
+    j = T.rank_of(core)
+    if j is None:
+        return
+    cnt = T.tables["CNT"]
+    n = len(T.cores)
+    S = T.sem
+    v, s, t, q = g.vector, g.scalar, g.tensor, g.sync
+
+    q.dma_start(T.xb[:, 0:4 * WIN], T.x[:, 0:4 * WIN]).then_inc(S.ldx0, 16)
+    s.dma_start(T.xb[:, 4 * WIN:4 * NC], T.x[:, 4 * WIN:4 * NC]).then_inc(S.ldx1, 16)
+    q.dma_start(T.w1b[:], T.w1[:]).then_inc(S.ldw1, 16)
+    s.dma_start(T.w2b[:], T.w2[:]).then_inc(S.ldw2, 16)
+
+    v.wait_ge(S.ldx0, 16)
+    v.quantize_mx(T.xq[:, 0:WIN], T.xs[:, 0:WIN], T.xb[:, 0:4 * WIN]).then_inc(S.qx0, 1)
+    v.wait_ge(S.ldx1, 16)
+    v.quantize_mx(T.xq[:, WIN:NC], T.xs[:, WIN:NC], T.xb[:, 4 * WIN:4 * NC]).then_inc(S.qx1, 1)
+    v.wait_ge(S.ldw1, 16)
+    v.quantize_mx(T.w1q[:], T.w1s[:], T.w1b[:]).then_inc(S.qw1, 1)
+    v.wait_ge(S.ldw2, 16)
+    v.quantize_mx(T.w2q[:], T.w2s[:], T.w2b[:]).then_inc(S.qw2, 1)
+
+    runs = _plan(cnt, j)
+    loads = []
+    for (e, a, c, d) in runs:
+        loads += [ROW + 4 * c, ROW + c]
+    side = _deal(loads)
+    g.wait_ge(S.qx0, 1)
+    second = False
+    sent = 0
+    for i, (e, a, c, d) in enumerate(runs):
+        if a + c > WIN and not second:
+            g.wait_ge(S.qx1, 1)
+            second = True
+        dst = T.cores[e]
+        assert topo.may_write(core, dst)
+        rid, pid, _ = topo.addr(dst)
+        grp, ne = _groups(topo.mask(core, dst), 2)
+        arr = S.arrA if d < WIN else S.arrB
+        g.remote_dma(out_ap=T.bq[:, d:d + c].bitcast(dt.uint8), in_ap=T.xq[:, a:a + c].bitcast(dt.uint8),
+                     remote_sem=arr, local_sem=S.sent, pid=pid, routing_id=rid, dma_engine_mask=grp[side[2 * i]])
+        g.remote_dma(out_ap=T.bs[:, d:d + c], in_ap=T.xs[:, a:a + c],
+                     remote_sem=arr, local_sem=S.sent, pid=pid, routing_id=rid, dma_engine_mask=grp[side[2 * i + 1]])
+        sent += 2 * ne
+    if not second:
+        g.wait_ge(S.qx1, 1)
+
+    tot = [0, 0]
+    for k in range(n):
+        if k != j and cnt[k][j]:
+            d = sum(cnt[m][j] for m in range(k))
+            ne = _groups(topo.mask(T.cores[k], core), 2)[1]
+            tot[0 if d < WIN else 1] += 2 * ne
+    own = cnt[j][j]
+    far = NC - own
+    assert own == 0 or (sum(cnt[k][j] for k in range(j)) == far and far >= WIN)
+    oa = sum(cnt[j][:j])
+    ow = min(oa, NC - WIN)
+    assert own == 0 or ow >= WIN
+
+    def bank(k, lo=0, hi=WIN):
+        return T.ps[:, k * BANK + lo:k * BANK + hi]
+
+    def w1t(b):
+        return T.w1q[:, 128 * b:128 * b + 128], T.w1s[:, 128 * b:128 * b + 128]
+
+    t.wait_ge(S.qw1, 1)
+    if own:
+        t.wait_ge(S.qx1, 1)
+        for b in range(G):
+            wq, ws = w1t(b)
+            t.matmul_mx(bank(G + b), wq, ws, T.xq[:, ow:ow + WIN], T.xs[:, ow:ow + WIN], True, True).then_inc(S["zo%d" % b], 1)
+    if tot[0]:
+        t.wait_ge(S.arrA, tot[0])
+    for b in range(G):
+        wq, ws = w1t(b)
+        t.matmul_mx(bank(b), wq, ws, T.bq[:, 0:WIN], T.bs[:, 0:WIN], True, True).then_inc(S["z0%d" % b], 1)
+    if tot[1]:
+        t.wait_ge(S.arrB, tot[1])
+    if own:
+        t.wait_ge(S.aown, G)
+    for b in range(G):
+        wq, ws = w1t(b)
+        t.matmul_mx(bank(G + b), wq, ws, T.bq[:, far - WIN:far], T.bs[:, far - WIN:far], True, True).then_inc(S["z1%d" % b], 1)
+    t.wait_ge(S.qw2, 1)
+    t.wait_ge(S.qh0, 1)
+    t.matmul_mx(bank(0), T.w2q[:], T.w2s[:], T.hq[:, 0:WIN], T.hs[:, 0:WIN], True, True).then_inc(S.p0, 1)
+    t.wait_ge(S.qh1, 1)
+    t.matmul_mx(bank(1), T.w2q[:], T.w2s[:], T.hq[:, WIN:NC], T.hs[:, WIN:NC], True, True).then_inc(S.p1, 1)
+
+    def act(b, src, c0, c1, done):
+        out = T.h[:, 4 * c0 + b:4 * c1:4]
+        if b % 2 == 0:
+            v.tensor_scalar(out, src, 0.0, C, AluOpType.max, AluOpType.mult).then_inc(done, 1)
+        else:
+            s.activation(out, src, ActivationFunctionType.Relu, scale=C).then_inc(done, 1)
+
+    def eng(b):
+        return v if b % 2 == 0 else s
+
+    if own:
+        for b in range(G):
+            eng(b).wait_ge(S["zo%d" % b], 1)
+            act(b, bank(G + b, oa - ow, oa - ow + own), far, NC, S.aown)
+    for b in range(G):
+        eng(b).wait_ge(S["z0%d" % b], 1)
+        act(b, bank(b), 0, WIN, S.a0)
+    v.wait_ge(S.a0, G)
+    v.quantize_mx(T.hq[:, 0:WIN], T.hs[:, 0:WIN], T.h[:, 0:4 * WIN]).then_inc(S.qh0, 1)
+    for b in range(G):
+        eng(b).wait_ge(S["z1%d" % b], 1)
+        act(b, bank(G + b, 2 * WIN - far, WIN), WIN, far, S.a1)
+    v.wait_ge(S.a1, G)
+    if own:
+        v.wait_ge(S.aown, G)
+    v.quantize_mx(T.hq[:, WIN:NC], T.hs[:, WIN:NC], T.h[:, 4 * WIN:4 * NC]).then_inc(S.qh1, 1)
+
+    s.wait_ge(S.p0, 1)
+    s.activation(T.ys[:, 0:WIN], bank(0), ActivationFunctionType.Copy).then_inc(S.c0, 1)
+    s.wait_ge(S.c0, 1)
+    s.dma_start(T.y[:, 0:WIN], T.ys[:, 0:WIN]).then_inc(S.st, 16)
+    v.wait_ge(S.p1, 1)
+    v.tensor_copy(T.ys[:, WIN:NC], bank(1)).then_inc(S.c1, 1)
+    q.wait_ge(S.c1, 1)
+    q.dma_start(T.y[:, WIN:NC], T.ys[:, WIN:NC]).then_inc(S.st, 16)
+    q.wait_ge(S.st, 32)
+    g.wait_ge(S.sent, sent)

@@ -5,7 +5,7 @@ WIN = 128
 G = 4
 C = 0.041
 BANK = 512
-ROW = 512
+ORDER = [[3, 1, 4], [2, 4, 0, 3], [4, 0, 3, 1], [1, 2, 0], [0, 3, 1, 2]]
 
 SCRATCH = {
     "xb": ("sbuf", [128, 4 * NC], "bfloat16"),
@@ -32,28 +32,45 @@ SEMAPHORES = (["ldx0", "ldx1", "ldw1", "ldw2", "qx0", "qx1", "qw1", "qw2", "arrA
 
 def _groups(mask, k):
     bits = [i for i in range(16) if (mask >> i) & 1]
-    n = len(bits) // k
-    return [sum(1 << i for i in bits[t * n:(t + 1) * n]) for t in range(k)], n
+    return [sum(1 << i for i in bits[t::k]) for t in range(k)], len(bits) // k
 
 
-def _deal(loads):
+def _sides(cs):
     best, pick = None, None
-    for m in range(1 << len(loads)):
-        s1 = sum(v for i, v in enumerate(loads) if (m >> i) & 1)
-        top = max(s1, sum(loads) - s1)
+    for m in range(0, 1 << len(cs), 2):
+        x = sum(c if (m >> i) & 1 else 4 * c for i, c in enumerate(cs))
+        top = max(x, 5 * sum(cs) - x)
         if best is None or top < best:
             best, pick = top, m
-    return [(pick >> i) & 1 for i in range(len(loads))]
+    out = []
+    for i in range(len(cs)):
+        out += [(pick >> i) & 1, 1 - ((pick >> i) & 1)]
+    return out
 
 
 def _plan(cnt, j):
-    n = len(cnt)
-    runs = []
-    for e in range(n):
-        if e != j and cnt[j][e]:
-            runs.append((e, sum(cnt[j][:e]), cnt[j][e], sum(cnt[k][e] for k in range(j))))
-    runs.sort(key=lambda r: (r[1] + r[2] > WIN, r[3] >= WIN, r[1]))
-    return runs
+    assert sorted(ORDER[j]) == [e for e in range(len(cnt)) if e != j and cnt[j][e]]
+    return [(e, sum(cnt[j][:e]), cnt[j][e], sum(cnt[k][e] for k in range(j))) for e in ORDER[j]]
+
+
+def _span(cnt, e, k):
+    far = NC - cnt[e][e]
+    return (0, WIN) if k == 0 else (far - WIN, far)
+
+
+def _touch(cnt, e, k):
+    lo, hi = _span(cnt, e, k)
+    out = []
+    for m in range(len(cnt)):
+        d = sum(cnt[i][e] for i in range(m))
+        if m != e and cnt[m][e] and d < hi and d + cnt[m][e] > lo:
+            out.append(m)
+    return out
+
+
+def _first(cnt, e):
+    late = [max(ORDER[m].index(e) for m in _touch(cnt, e, k)) for k in range(2)]
+    return 0 if late[0] <= late[1] else 1
 
 
 def rank_program(g, core, T, topo):
@@ -65,51 +82,55 @@ def rank_program(g, core, T, topo):
     S = T.sem
     v, s, t, q = g.vector, g.scalar, g.tensor, g.sync
 
-    q.dma_start(T.xb[:, 0:4 * WIN], T.x[:, 0:4 * WIN]).then_inc(S.ldx0, 16)
-    s.dma_start(T.xb[:, 4 * WIN:4 * NC], T.x[:, 4 * WIN:4 * NC]).then_inc(S.ldx1, 16)
+    runs = _plan(cnt, j)
+    hf = 1 if runs[0][1] >= WIN else 0
+    halves = [hf, 1 - hf]
+
+    def xcols(hh, m):
+        return slice(m * WIN * hh, m * WIN * (hh + 1))
+
+    q.dma_start(T.xb[:, xcols(halves[0], 4)], T.x[:, xcols(halves[0], 4)]).then_inc(S["ldx%d" % halves[0]], 16)
+    s.dma_start(T.xb[:, xcols(halves[1], 4)], T.x[:, xcols(halves[1], 4)]).then_inc(S["ldx%d" % halves[1]], 16)
     q.dma_start(T.w1b[:], T.w1[:]).then_inc(S.ldw1, 16)
     s.dma_start(T.w2b[:], T.w2[:]).then_inc(S.ldw2, 16)
 
-    v.wait_ge(S.ldx0, 16)
-    v.quantize_mx(T.xq[:, 0:WIN], T.xs[:, 0:WIN], T.xb[:, 0:4 * WIN]).then_inc(S.qx0, 1)
-    v.wait_ge(S.ldx1, 16)
-    v.quantize_mx(T.xq[:, WIN:NC], T.xs[:, WIN:NC], T.xb[:, 4 * WIN:4 * NC]).then_inc(S.qx1, 1)
+    for hh in halves:
+        v.wait_ge(S["ldx%d" % hh], 16)
+        v.quantize_mx(T.xq[:, xcols(hh, 1)], T.xs[:, xcols(hh, 1)], T.xb[:, xcols(hh, 4)]).then_inc(S["qx%d" % hh], 1)
     v.wait_ge(S.ldw1, 16)
     v.quantize_mx(T.w1q[:], T.w1s[:], T.w1b[:]).then_inc(S.qw1, 1)
     v.wait_ge(S.ldw2, 16)
     v.quantize_mx(T.w2q[:], T.w2s[:], T.w2b[:]).then_inc(S.qw2, 1)
 
-    runs = _plan(cnt, j)
-    loads = []
-    for (e, a, c, d) in runs:
-        loads += [ROW + 4 * c, ROW + c]
-    side = _deal(loads)
-    g.wait_ge(S.qx0, 1)
-    second = False
+    side = _sides([r[2] for r in runs])
+    have = set()
     sent = 0
     for i, (e, a, c, d) in enumerate(runs):
-        if a + c > WIN and not second:
-            g.wait_ge(S.qx1, 1)
-            second = True
+        for hh in halves:
+            if hh not in have and a < WIN * (hh + 1) and a + c > WIN * hh:
+                g.wait_ge(S["qx%d" % hh], 1)
+                have.add(hh)
         dst = T.cores[e]
         assert topo.may_write(core, dst)
         rid, pid, _ = topo.addr(dst)
         grp, ne = _groups(topo.mask(core, dst), 2)
-        arr = S.arrA if d < WIN else S.arrB
+        arr = S.arrA if j in _touch(cnt, e, _first(cnt, e)) else S.arrB
         g.remote_dma(out_ap=T.bq[:, d:d + c].bitcast(dt.uint8), in_ap=T.xq[:, a:a + c].bitcast(dt.uint8),
                      remote_sem=arr, local_sem=S.sent, pid=pid, routing_id=rid, dma_engine_mask=grp[side[2 * i]])
         g.remote_dma(out_ap=T.bs[:, d:d + c], in_ap=T.xs[:, a:a + c],
                      remote_sem=arr, local_sem=S.sent, pid=pid, routing_id=rid, dma_engine_mask=grp[side[2 * i + 1]])
         sent += 2 * ne
-    if not second:
-        g.wait_ge(S.qx1, 1)
+    for hh in halves:
+        if hh not in have:
+            g.wait_ge(S["qx%d" % hh], 1)
 
+    order = [_first(cnt, j), 1 - _first(cnt, j)]
+    early = _touch(cnt, j, order[0])
     tot = [0, 0]
     for k in range(n):
         if k != j and cnt[k][j]:
-            d = sum(cnt[m][j] for m in range(k))
             ne = _groups(topo.mask(T.cores[k], core), 2)[1]
-            tot[0 if d < WIN else 1] += 2 * ne
+            tot[0 if k in early else 1] += 2 * ne
     own = cnt[j][j]
     far = NC - own
     assert own == 0 or (sum(cnt[k][j] for k in range(j)) == far and far >= WIN)
@@ -129,23 +150,20 @@ def rank_program(g, core, T, topo):
         for b in range(G):
             wq, ws = w1t(b)
             t.matmul_mx(bank(G + b), wq, ws, T.xq[:, ow:ow + WIN], T.xs[:, ow:ow + WIN], True, True).then_inc(S["zo%d" % b], 1)
-    if tot[0]:
-        t.wait_ge(S.arrA, tot[0])
-    for b in range(G):
-        wq, ws = w1t(b)
-        t.matmul_mx(bank(b), wq, ws, T.bq[:, 0:WIN], T.bs[:, 0:WIN], True, True).then_inc(S["z0%d" % b], 1)
-    if tot[1]:
-        t.wait_ge(S.arrB, tot[1])
-    if own:
-        t.wait_ge(S.aown, G)
-    for b in range(G):
-        wq, ws = w1t(b)
-        t.matmul_mx(bank(G + b), wq, ws, T.bq[:, far - WIN:far], T.bs[:, far - WIN:far], True, True).then_inc(S["z1%d" % b], 1)
+    for i, k in enumerate(order):
+        if tot[i]:
+            t.wait_ge(S.arrA if i == 0 else S.arrB, tot[i])
+        if k == 1 and own:
+            t.wait_ge(S.aown, G)
+        lo, hi = _span(cnt, j, k)
+        for b in range(G):
+            wq, ws = w1t(b)
+            t.matmul_mx(bank(G * k + b), wq, ws, T.bq[:, lo:hi], T.bs[:, lo:hi], True, True).then_inc(S["z%d%d" % (k, b)], 1)
     t.wait_ge(S.qw2, 1)
-    t.wait_ge(S.qh0, 1)
-    t.matmul_mx(bank(0), T.w2q[:], T.w2s[:], T.hq[:, 0:WIN], T.hs[:, 0:WIN], True, True).then_inc(S.p0, 1)
-    t.wait_ge(S.qh1, 1)
-    t.matmul_mx(bank(1), T.w2q[:], T.w2s[:], T.hq[:, WIN:NC], T.hs[:, WIN:NC], True, True).then_inc(S.p1, 1)
+    for k in order:
+        t.wait_ge(S["qh%d" % k], 1)
+        t.matmul_mx(bank(G * k), T.w2q[:], T.w2s[:], T.hq[:, WIN * k:WIN * k + WIN], T.hs[:, WIN * k:WIN * k + WIN],
+                    True, True).then_inc(S["p%d" % k], 1)
 
     def act(b, src, c0, c1, done):
         out = T.h[:, 4 * c0 + b:4 * c1:4]
@@ -161,26 +179,27 @@ def rank_program(g, core, T, topo):
         for b in range(G):
             eng(b).wait_ge(S["zo%d" % b], 1)
             act(b, bank(G + b, oa - ow, oa - ow + own), far, NC, S.aown)
-    for b in range(G):
-        eng(b).wait_ge(S["z0%d" % b], 1)
-        act(b, bank(b), 0, WIN, S.a0)
-    v.wait_ge(S.a0, G)
-    v.quantize_mx(T.hq[:, 0:WIN], T.hs[:, 0:WIN], T.h[:, 0:4 * WIN]).then_inc(S.qh0, 1)
-    for b in range(G):
-        eng(b).wait_ge(S["z1%d" % b], 1)
-        act(b, bank(G + b, 2 * WIN - far, WIN), WIN, far, S.a1)
-    v.wait_ge(S.a1, G)
-    if own:
-        v.wait_ge(S.aown, G)
-    v.quantize_mx(T.hq[:, WIN:NC], T.hs[:, WIN:NC], T.h[:, 4 * WIN:4 * NC]).then_inc(S.qh1, 1)
+    for k in order:
+        for b in range(G):
+            eng(b).wait_ge(S["z%d%d" % (k, b)], 1)
+            if k == 0:
+                act(b, bank(b), 0, WIN, S.a0)
+            else:
+                act(b, bank(G + b, 2 * WIN - far, WIN), WIN, far, S.a1)
+        v.wait_ge(S["a%d" % k], G)
+        if k == 1 and own:
+            v.wait_ge(S.aown, G)
+        v.quantize_mx(T.hq[:, WIN * k:WIN * k + WIN], T.hs[:, WIN * k:WIN * k + WIN],
+                      T.h[:, 4 * WIN * k:4 * WIN * (k + 1)]).then_inc(S["qh%d" % k], 1)
 
-    s.wait_ge(S.p0, 1)
-    s.activation(T.ys[:, 0:WIN], bank(0), ActivationFunctionType.Copy).then_inc(S.c0, 1)
+    k0, k1 = order
+    s.wait_ge(S["p%d" % k0], 1)
+    s.activation(T.ys[:, WIN * k0:WIN * k0 + WIN], bank(G * k0), ActivationFunctionType.Copy).then_inc(S.c0, 1)
     s.wait_ge(S.c0, 1)
-    s.dma_start(T.y[:, 0:WIN], T.ys[:, 0:WIN]).then_inc(S.st, 16)
-    v.wait_ge(S.p1, 1)
-    v.tensor_copy(T.ys[:, WIN:NC], bank(1)).then_inc(S.c1, 1)
+    s.dma_start(T.y[:, WIN * k0:WIN * k0 + WIN], T.ys[:, WIN * k0:WIN * k0 + WIN]).then_inc(S.st, 16)
+    v.wait_ge(S["p%d" % k1], 1)
+    v.tensor_copy(T.ys[:, WIN * k1:WIN * k1 + WIN], bank(G * k1)).then_inc(S.c1, 1)
     q.wait_ge(S.c1, 1)
-    q.dma_start(T.y[:, WIN:NC], T.ys[:, WIN:NC]).then_inc(S.st, 16)
+    q.dma_start(T.y[:, WIN * k1:WIN * k1 + WIN], T.ys[:, WIN * k1:WIN * k1 + WIN]).then_inc(S.st, 16)
     q.wait_ge(S.st, 32)
     g.wait_ge(S.sent, sent)

from concourse.mybir import dt, AluOpType, ActivationFunctionType

NC = 256
WIN = 128
G = 4
C = 0.041
BANK = 512
ORDER = [[3, 1, 4], [2, 4, 0, 3], [4, 0, 3, 1], [1, 2, 0], [0, 3, 1, 2]]

SCRATCH = {
    "xb": ("sbuf", [128, 4 * NC], "bfloat16"),
    "w1b": ("sbuf", [128, G * 512], "bfloat16"),
    "w2b": ("sbuf", [128, 512], "bfloat16"),
    "xq": ("sbuf", [128, NC], "float8_e4m3fn_x4"),
    "xs": ("sbuf", [128, NC], "uint8"),
    "w1q": ("sbuf", [128, G * 128], "float8_e4m3fn_x4"),
    "w1s": ("sbuf", [128, G * 128], "uint8"),
    "w2q": ("sbuf", [128, 128], "float8_e4m3fn_x4"),
    "w2s": ("sbuf", [128, 128], "uint8"),
    "bq": ("sbuf", [128, NC], "float8_e4m3fn_x4"),
    "bs": ("sbuf", [128, NC], "uint8"),
    "h": ("sbuf", [128, 4 * NC], "bfloat16"),
    "hq": ("sbuf", [128, NC], "float8_e4m3fn_x4"),
    "hs": ("sbuf", [128, NC], "uint8"),
    "ys": ("sbuf", [128, NC], "float32"),
    "ps": ("psum", [128, 8 * BANK], "float32"),
}
SEMAPHORES = (["ldx0", "ldx1", "ldw1", "ldw2", "qx0", "qx1", "qw1", "qw2", "arrA", "arrB", "sent",
               "a0", "a1", "aown", "qh0", "qh1", "p0", "p1", "c0", "c1", "st"]
              + ["z0%d" % b for b in range(G)] + ["z1%d" % b for b in range(G)] + ["zo%d" % b for b in range(G)])


def _groups(mask, k):
    bits = [i for i in range(16) if (mask >> i) & 1]
    return [sum(1 << i for i in bits[t::k]) for t in range(k)], len(bits) // k


def _sides(cs):
    best, pick = None, None
    for m in range(0, 1 << len(cs), 2):
        x = sum(c if (m >> i) & 1 else 4 * c for i, c in enumerate(cs))
        top = max(x, 5 * sum(cs) - x)
        if best is None or top < best:
            best, pick = top, m
    out = []
    for i in range(len(cs)):
        out += [(pick >> i) & 1, 1 - ((pick >> i) & 1)]
    return out


def _plan(cnt, j):
    assert sorted(ORDER[j]) == [e for e in range(len(cnt)) if e != j and cnt[j][e]]
    return [(e, sum(cnt[j][:e]), cnt[j][e], sum(cnt[k][e] for k in range(j))) for e in ORDER[j]]


def _span(cnt, e, k):
    far = NC - cnt[e][e]
    return (0, WIN) if k == 0 else (far - WIN, far)


def _touch(cnt, e, k):
    lo, hi = _span(cnt, e, k)
    out = []
    for m in range(len(cnt)):
        d = sum(cnt[i][e] for i in range(m))
        if m != e and cnt[m][e] and d < hi and d + cnt[m][e] > lo:
            out.append(m)
    return out


def _first(cnt, e):
    late = [max(ORDER[m].index(e) for m in _touch(cnt, e, k)) for k in range(2)]
    return 0 if late[0] <= late[1] else 1


def rank_program(g, core, T, topo):
    j = T.rank_of(core)
    if j is None:
        return
    cnt = T.tables["CNT"]
    n = len(T.cores)
    S = T.sem
    v, s, t, q = g.vector, g.scalar, g.tensor, g.sync

    runs = _plan(cnt, j)
    hf = 1 if runs[0][1] >= WIN else 0
    halves = [hf, 1 - hf]

    def xcols(hh, m):
        return slice(m * WIN * hh, m * WIN * (hh + 1))

    q.dma_start(T.xb[:, xcols(halves[0], 4)], T.x[:, xcols(halves[0], 4)]).then_inc(S["ldx%d" % halves[0]], 16)
    s.dma_start(T.xb[:, xcols(halves[1], 4)], T.x[:, xcols(halves[1], 4)]).then_inc(S["ldx%d" % halves[1]], 16)
    q.dma_start(T.w1b[:], T.w1[:]).then_inc(S.ldw1, 16)
    s.dma_start(T.w2b[:], T.w2[:]).then_inc(S.ldw2, 16)

    for hh in halves:
        v.wait_ge(S["ldx%d" % hh], 16)
        v.quantize_mx(T.xq[:, xcols(hh, 1)], T.xs[:, xcols(hh, 1)], T.xb[:, xcols(hh, 4)]).then_inc(S["qx%d" % hh], 1)
    v.wait_ge(S.ldw1, 16)
    v.quantize_mx(T.w1q[:], T.w1s[:], T.w1b[:]).then_inc(S.qw1, 1)
    v.wait_ge(S.ldw2, 16)
    v.quantize_mx(T.w2q[:], T.w2s[:], T.w2b[:]).then_inc(S.qw2, 1)

    side = _sides([r[2] for r in runs])
    have = set()
    sent = 0
    for i, (e, a, c, d) in enumerate(runs):
        for hh in halves:
            if hh not in have and a < WIN * (hh + 1) and a + c > WIN * hh:
                g.wait_ge(S["qx%d" % hh], 1)
                have.add(hh)
        dst = T.cores[e]
        assert topo.may_write(core, dst)
        rid, pid, _ = topo.addr(dst)
        grp, ne = _groups(topo.mask(core, dst), 2)
        arr = S.arrA if j in _touch(cnt, e, _first(cnt, e)) else S.arrB
        g.remote_dma(out_ap=T.bq[:, d:d + c].bitcast(dt.uint8), in_ap=T.xq[:, a:a + c].bitcast(dt.uint8),
                     remote_sem=arr, local_sem=S.sent, pid=pid, routing_id=rid, dma_engine_mask=grp[side[2 * i]])
        g.remote_dma(out_ap=T.bs[:, d:d + c], in_ap=T.xs[:, a:a + c],
                     remote_sem=arr, local_sem=S.sent, pid=pid, routing_id=rid, dma_engine_mask=grp[side[2 * i + 1]])
        sent += 2 * ne
    for hh in halves:
        if hh not in have:
            g.wait_ge(S["qx%d" % hh], 1)

    order = [_first(cnt, j), 1 - _first(cnt, j)]
    early = _touch(cnt, j, order[0])
    tot = [0, 0]
    for k in range(n):
        if k != j and cnt[k][j]:
            ne = _groups(topo.mask(T.cores[k], core), 2)[1]
            tot[0 if k in early else 1] += 2 * ne
    own = cnt[j][j]
    far = NC - own
    assert own == 0 or (sum(cnt[k][j] for k in range(j)) == far and far >= WIN)
    oa = sum(cnt[j][:j])
    ow = min(oa, NC - WIN)
    assert own == 0 or ow >= WIN

    def bank(k, lo=0, hi=WIN):
        return T.ps[:, k * BANK + lo:k * BANK + hi]

    def w1t(b):
        return T.w1q[:, 128 * b:128 * b + 128], T.w1s[:, 128 * b:128 * b + 128]

    t.wait_ge(S.qw1, 1)
    if own:
        t.wait_ge(S.qx1, 1)
        for b in range(G):
            wq, ws = w1t(b)
            t.matmul_mx(bank(G + b), wq, ws, T.xq[:, ow:ow + WIN], T.xs[:, ow:ow + WIN], True, True).then_inc(S["zo%d" % b], 1)
    for i, k in enumerate(order):
        if tot[i]:
            t.wait_ge(S.arrA if i == 0 else S.arrB, tot[i])
        if k == 1 and own:
            t.wait_ge(S.aown, G)
        lo, hi = _span(cnt, j, k)
        for b in range(G):
            wq, ws = w1t(b)
            t.matmul_mx(bank(G * k + b), wq, ws, T.bq[:, lo:hi], T.bs[:, lo:hi], True, True).then_inc(S["z%d%d" % (k, b)], 1)
    t.wait_ge(S.qw2, 1)
    for k in order:
        t.wait_ge(S["qh%d" % k], 1)
        t.matmul_mx(bank(G * k), T.w2q[:], T.w2s[:], T.hq[:, WIN * k:WIN * k + WIN], T.hs[:, WIN * k:WIN * k + WIN],
                    True, True).then_inc(S["p%d" % k], 1)

    def act(b, src, c0, c1, done):
        out = T.h[:, 4 * c0 + b:4 * c1:4]
        if b % 2 == 0:
            v.tensor_scalar(out, src, 0.0, C, AluOpType.max, AluOpType.mult).then_inc(done, 1)
        else:
            s.activation(out, src, ActivationFunctionType.Relu, scale=C).then_inc(done, 1)

    def eng(b):
        return v if b % 2 == 0 else s

    if own:
        for b in range(G):
            eng(b).wait_ge(S["zo%d" % b], 1)
            act(b, bank(G + b, oa - ow, oa - ow + own), far, NC, S.aown)
    for k in order:
        for b in range(G):
            eng(b).wait_ge(S["z%d%d" % (k, b)], 1)
            if k == 0:
                act(b, bank(b), 0, WIN, S.a0)
            else:
                act(b, bank(G + b, 2 * WIN - far, WIN), WIN, far, S.a1)
        v.wait_ge(S["a%d" % k], G)
        if k == 1 and own:
            v.wait_ge(S.aown, G)
        v.quantize_mx(T.hq[:, WIN * k:WIN * k + WIN], T.hs[:, WIN * k:WIN * k + WIN],
                      T.h[:, 4 * WIN * k:4 * WIN * (k + 1)]).then_inc(S["qh%d" % k], 1)

    k0, k1 = order
    s.wait_ge(S["p%d" % k0], 1)
    s.activation(T.ys[:, WIN * k0:WIN * k0 + WIN], bank(G * k0), ActivationFunctionType.Copy).then_inc(S.c0, 1)
    s.wait_ge(S.c0, 1)
    s.dma_start(T.y[:, WIN * k0:WIN * k0 + WIN], T.ys[:, WIN * k0:WIN * k0 + WIN]).then_inc(S.st, 16)
    v.wait_ge(S["p%d" % k1], 1)
    v.tensor_copy(T.ys[:, WIN * k1:WIN * k1 + WIN], bank(G * k1)).then_inc(S.c1, 1)
    q.wait_ge(S.c1, 1)
    q.dma_start(T.y[:, WIN * k1:WIN * k1 + WIN], T.ys[:, WIN * k1:WIN * k1 + WIN]).then_inc(S.st, 16)
    q.wait_ge(S.st, 32)
    g.wait_ge(S.sent, sent)
